import numpy as np
import ml_dtypes


def mxq(x, axis, fmt="e4m3"):
    dtype, down = {"e4m3": (ml_dtypes.float8_e4m3fn, 7), "e5m2": (ml_dtypes.float8_e5m2, 14)}[fmt]
    v = np.moveaxis(np.asarray(x, np.float32).astype(ml_dtypes.bfloat16).astype(np.float64), axis, -1)
    blocks = v.reshape(v.shape[:-1] + (-1, 32))
    amax = np.abs(blocks).max(-1, keepdims=True)
    byte = np.maximum(np.where(amax > 0, np.frexp(amax)[1] - 1 + 127, 0) - down, 1)
    scale = np.exp2(byte - 127.0)
    codes = (blocks / scale).astype(np.float32).astype(dtype).astype(np.float64)
    return np.moveaxis((codes * scale).reshape(v.shape), -1, axis)


WIDE = False


def mx_kscale(k):
    if not WIDE:
        return np.ones(k)
    levels = np.array([10, -10, 5, -5, 0])
    if k % 512:
        return np.exp2(np.random.permutation(np.resize(levels, k // 32))).repeat(32)
    a = np.empty((k // 512, 16))
    for p in range(k // 512):
        a[p, :8] = np.random.permutation(np.resize(levels, 8))
        for g in range(8):
            far = levels[np.abs(levels - a[p, g]) >= 10]
            a[p, g + 8] = far[np.random.randint(len(far))]
    return np.exp2(a.ravel()).repeat(32)


def f64(x):
    return np.asarray(x).astype(np.float64)


def striped(idx):
    return np.tile(idx.reshape(-1, 16).T, (8, 1)).astype(np.uint16)


def unstriped(offs):
    return offs[:16].T.reshape(-1).astype(np.int64)


def striped8(idx):
    return np.concatenate([x.reshape(-1, 16).T for x in idx]).astype(np.uint16)


def runs(offs, k):
    lists = np.stack([offs[16 * r : 16 * r + 16].T.reshape(-1) for r in range(8)]).astype(np.int64)
    return lists[np.arange(k) % 512 // 64]


def pack_weight(w):
    k, n = w.shape
    w = f64(np.asarray(w, np.float32).astype(ml_dtypes.bfloat16)).reshape(k // 32, 32, n)
    amax = np.abs(w).max(1)
    byte = np.clip(np.where(amax > 0, np.frexp(amax)[1] - 1 + 127 - 7, 1), 1, 254)
    scaled = (w * np.exp2(127.0 - byte)[:, None, :]).reshape(k, n).astype(np.float32)
    words = np.ascontiguousarray(scaled.reshape(k // 512, 128, 4, n).transpose(0, 1, 3, 2)).astype(ml_dtypes.float8_e4m3fn).view(np.uint8)
    return words, np.ascontiguousarray(byte.astype(np.uint8).reshape(k // 512, 16, n))


def unpack_weight(words, scales):
    g, p, n, _ = words.shape
    vals = np.ascontiguousarray(words).view(ml_dtypes.float8_e4m3fn).astype(np.float64) * np.repeat(np.exp2(scales.astype(np.float64) - 127.0), 8, axis=1)[..., None]
    return vals.transpose(0, 1, 3, 2).reshape(g * 512, n)


def sigmoid(v):
    return 1.0 / (1.0 + np.exp(-np.maximum(v, -700.0)))


K, T, S, H, U = 512, 2048, 512, 512, 1024


def setup_inputs():
    n = np.random.standard_normal
    s = mx_kscale(K)[:, None]
    u = mx_kscale(S)
    packed_xT = pack_weight(n((K, T)) * s)
    return {
        "x_words": packed_xT[0],
        "x_scales": packed_xT[1],
        "wa": (n((K, H)) / np.sqrt(K) / s).astype(np.float32),
        "wb": (n((K, H)) / np.sqrt(K) / s).astype(np.float32),
        "gt": (np.random.uniform(0.5, 1.5, (S, 1)) * u[:, None]).astype(np.float32),
        "gi": (np.random.uniform(0.5, 1.5, (S, 1)) / u[:, None]).astype(np.float32),
        "mem": n((H, U)).astype(np.float32),
        "offs": striped(np.random.permutation(T)[:S]),
        "two": striped(np.random.permutation(T)[:S]),
        "n1": striped8(np.stack([np.random.permutation(H) for _ in range(8)])),
        "n2": striped8(np.stack([np.random.permutation(H) for _ in range(8)])),
        "n3": striped8(np.stack([np.random.permutation(U)[:H] for _ in range(8)])),
    }


def reference(x_words, x_scales, wa, wb, gt, gi, mem, offs, two, n1, n2, n3):
    xq = unpack_weight(x_words, x_scales)[:, unstriped(offs)]
    a = xq.T @ mxq(f64(wa), 0, "e4m3")
    x_two = unpack_weight(x_words, x_scales)[:, unstriped(two)]
    b = x_two.T @ mxq(f64(wb), 0, "e4m3")
    z = f64(gt) * ((a + a[np.arange(S)[:, None], runs(n1, S)]) * (sigmoid(b + b[np.arange(S)[:, None], runs(n2, S)])))
    z2 = f64(gi) * b
    cv = 0.0625 * ((mxq(z, 0, "e4m3").T @ mxq(z2, 0, "e4m3")))
    nw = np.maximum(cv, 0.5 * (f64(mem)[np.arange(H)[:, None], runs(n3, H)]))
    out = f64(mem).copy()
    out[np.arange(H)[:, None], runs(n3, H)] = nw
    return out

@@ -1,0 +1,171 @@
+from contextlib import ExitStack
+
+import concourse.mybir as mybir
+
+F32 = mybir.dt.float32
+BF16 = mybir.dt.bfloat16
+I32 = mybir.dt.int32
+U32 = mybir.dt.uint32
+U16 = mybir.dt.uint16
+U8 = mybir.dt.uint8
+FP8X4 = mybir.dt.float8_e4m3fn_x4
+ALU = mybir.AluOpType
+ACT = mybir.ActivationFunctionType
+
+P = 128
+PACK = 4
+K, T, S, H, U = 512, 2048, 512, 512, 1024
+HALF = H // 2
+FLOPS = 2 * (2 * K * S * H + S * H * H)
+
+
+def tile_picked_momttriebpagex_none_p_kernel(tc, x_words, x_scales, wa, wb, gt, gi, mem, offs, two, n1, n2, n3, out):
+    nc = tc.nc
+    with ExitStack() as ctx:
+        lists = ctx.enter_context(tc.tile_pool(name="lists", bufs=1))
+        keep = ctx.enter_context(tc.tile_pool(name="keep", bufs=1))
+        psum = ctx.enter_context(tc.psum_pool(name="psum", bufs=1))
+
+        def load_list(src, name):
+            tile = lists.tile([P, S // 16], U16, name=name)
+            nc.sync.dma_start(tile[:], src)
+            return tile
+
+        def load_weight_half(w, h, name):
+            raw = keep.tile([P, PACK, HALF], F32, name=name)
+            nc.sync.dma_start(raw[:], w.rearrange("(p j) c -> p j c", j=PACK)[:, :, h * HALF:(h + 1) * HALF])
+            return raw
+
+        def load_column(v, name):
+            tile = keep.tile([P, PACK], F32, name=name)
+            nc.sync.dma_start(tile[:], v.rearrange("(p t) o -> p (t o)", t=PACK))
+            return tile
+
+        scales_in = keep.tile([P, T], U8, name="scales_in", align_bytes=64)
+        nc.vector.memset(scales_in[:].bitcast(I32), 0)
+        two_l = load_list(two, "two_l")
+        offs_l = load_list(offs, "offs_l")
+        for q in range(4):
+            nc.scalar.dma_start(scales_in[32 * q:32 * q + 4, :].bitcast(I32), x_scales[0, 4 * q:4 * q + 4, :].bitcast(I32))
+        words_in = keep.tile([P, T], U32, name="words_in", align_bytes=64)
+        nc.sync.dma_start(words_in[:].bitcast(I32), x_words[0].rearrange("p n t -> p (n t)").bitcast(I32))
+        wb_raw = [load_weight_half(wb, h, "wb_raw%d" % h) for h in range(2)]
+        wa_raw = [load_weight_half(wa, h, "wa_raw%d" % h) for h in range(2)]
+        n2_l = load_list(n2, "n2_l")
+        gi_t = load_column(gi, "gi_t")
+        gt_t = load_column(gt, "gt_t")
+        n1_l = load_list(n1, "n1_l")
+        n3_l = load_list(n3, "n3_l")
+        page = []
+        for u in range(PACK):
+            tile = keep.tile([P, U], F32, name="page%d" % u)
+            nc.sync.dma_start(tile[:], mem.rearrange("(p u) w -> u p w", u=PACK)[u])
+            page.append(tile)
+
+        def pick(table, dtype, offsets, name, tag=None):
+            picked = keep.tile([P, S], dtype, name=name, tag=tag or name, align_bytes=64)
+            nc.vector.tensor_copy(picked[:].rearrange("p (t m) -> p m t", t=PACK), table[:].indirect(offsets[:]))
+            return picked
+
+        def interleave(copy, src, name, tag=None):
+            width = src.shape[2]
+            grouped = keep.tile([P, width * PACK], BF16, name=name, tag=tag or name, align_bytes=64)
+            copy(grouped[:].rearrange("p (c i t) -> p c t i", i=4, t=PACK), src.rearrange("p t (c i) -> p c t i", i=4))
+            return grouped
+
+        def mx_pair(name):
+            return (keep.tile([P, H], U32, name=name + "_codes", align_bytes=64),
+                    keep.tile([P, H], U8, name=name + "_scales", align_bytes=64))
+
+        def quantize(pair, cols, grouped):
+            nc.vector.quantize_mx(out=pair[0][:, cols].bitcast(FP8X4), scales=pair[1][:, cols], in_=grouped)
+
+        def product(acc, lhs, lhs_cols, rhs, rhs_cols):
+            nc.tensor.matmul_mx(out=acc, lhsT=lhs[0][:, lhs_cols].bitcast(FP8X4), lhsT_scale=lhs[1][:, lhs_cols],
+                                rhs=rhs[0][:, rhs_cols].bitcast(FP8X4), rhs_scale=rhs[1][:, rhs_cols], start=True, stop=True)
+
+        halves = [slice(h * HALF, (h + 1) * HALF) for h in range(2)]
+        blocks = [slice(t * P, (t + 1) * P) for t in range(PACK)]
+        whole = slice(0, H)
+
+        xb_scales = pick(scales_in, U8, two_l, "xb_scales")
+        xa_scales = pick(scales_in, U8, offs_l, "xa_scales")
+        xb = (pick(words_in, U32, two_l, "xb_words"), xb_scales)
+        wb_q = mx_pair("wb")
+        wb_g = [interleave(nc.scalar.copy, wb_raw[0][:], "wb_g0"), interleave(nc.vector.tensor_copy, wb_raw[1][:], "wb_g1")]
+        for h in range(2):
+            nc.vector.quantize_mx(out=wb_q[0][:, halves[h]].bitcast(FP8X4), scales=wb_q[1][4 * h:P, halves[0]], in_=wb_g[h][:])
+        b_acc = [psum.tile([P, H], F32, name="b_acc%d" % t, tag="bank%d" % t) for t in range(PACK)]
+        for t in range(PACK):
+            for h in range(2):
+                nc.tensor.matmul_mx(out=b_acc[t][:, halves[h]], lhsT=xb[0][:, blocks[t]].bitcast(FP8X4), lhsT_scale=xb[1][:, blocks[t]],
+                                    rhs=wb_q[0][:, halves[h]].bitcast(FP8X4), rhs_scale=wb_q[1][4 * h:P, halves[0]], start=True, stop=True)
+        xa = (pick(words_in, U32, offs_l, "xa_words", "wb_g1"), xa_scales)
+
+        b_row = [keep.tile([P, H], F32, name="b_row%d" % t) for t in range(PACK)]
+        for t in range(PACK):
+            nc.scalar.copy(b_row[t][:], b_acc[t][:])
+
+        wa_q = mx_pair("wa")
+        wa_g = keep.tile([P, H * PACK], BF16, name="wa_g", tag="wb_g0", align_bytes=64)
+        for h in range(2):
+            nc.vector.tensor_copy(wa_g[:, h * HALF * PACK:(h + 1) * HALF * PACK].rearrange("p (c i t) -> p c t i", i=4, t=PACK),
+                                  wa_raw[h][:].rearrange("p t (c i) -> p c t i", i=4))
+        quantize(wa_q, whole, wa_g[:])
+        a_acc = [psum.tile([P, H], F32, name="a_acc%d" % t, tag="bank%d" % (PACK + t)) for t in range(PACK)]
+        for t in range(PACK):
+            product(a_acc[t][:], xa, blocks[t], wa_q, whole)
+
+        def fetch(on_vector, dst, row, offsets, h):
+            window = row[:].indirect(offsets[:, 16 * h:16 * (h + 1)])
+            if on_vector:
+                nc.vector.tensor_copy(dst[:, halves[h]], window)
+            else:
+                nc.scalar.activation(dst[:, halves[h]], window, ACT.Copy)
+
+        gate = keep.tile([P, PACK, H], F32, name="gate")
+        z2_rows = keep.tile([P, PACK, H], BF16, name="z2_rows")
+        b_sum = [keep.tile([P, H], F32, name="b_sum%d" % t) for t in range(PACK)]
+        a_row = [keep.tile([P, H], F32, name="a_row%d" % t, tag="a_row%d" % t) for t in range(PACK)]
+        for t in range(2):
+            for h in range(2):
+                fetch(False, b_sum[t], b_row[t], n2_l, h)
+            for h in range(2):
+                fetch(True, b_sum[t + 2], b_row[t + 2], n2_l, h)
+            nc.vector.tensor_tensor(b_sum[t][:], b_acc[t][:], b_sum[t][:], ALU.add)
+        for t in range(2, PACK):
+            nc.vector.tensor_tensor(b_sum[t][:], b_acc[t][:], b_sum[t][:], ALU.add)
+        for t in range(PACK):
+            nc.scalar.activation(a_row[t][:], a_acc[t][:], ACT.Copy, scale=gt_t[:, t:t + 1])
+        for t in range(PACK):
+            nc.scalar.activation(gate[:, t, :], b_sum[t][:], ACT.Sigmoid)
+        for t in range(PACK):
+            nc.vector.tensor_scalar(z2_rows[:, t, :], b_row[t][:], gi_t[:, t:t + 1], None, ALU.mult)
+        z2_g = interleave(nc.vector.tensor_copy, z2_rows[:], "z2_g")
+        z2_q = mx_pair("z2")
+        quantize(z2_q, whole, z2_g[:])
+
+        a_got = [keep.tile([P, H], F32, name="a_got%d" % t) for t in range(PACK)]
+        a_sum = keep.tile([P, PACK, H], F32, name="a_sum")
+        z_g = keep.tile([P, PACK, P, PACK], BF16, name="z_g", align_bytes=64)
+        for h in range(2):
+            for t in range(PACK):
+                fetch(h == 0 and t == 0, a_got[t], a_row[t], n1_l, h)
+                nc.vector.scalar_tensor_tensor(a_sum[:, t, halves[h]], a_acc[t][:, halves[h]], gt_t[:, t:t + 1],
+                                               a_got[t][:, halves[h]], ALU.mult, ALU.add)
+            nc.vector.tensor_tensor(z_g[:, :, 64 * h:64 * (h + 1), :].rearrange("p u m t -> p m t u"),
+                                    a_sum[:, :, halves[h]].rearrange("p t (m u) -> p m t u", u=PACK),
+                                    gate[:, :, halves[h]].rearrange("p t (m u) -> p m t u", u=PACK), ALU.mult)
+
+        z_q = mx_pair("z")
+        cv_acc = [psum.tile([P, H], F32, name="cv_acc%d" % u, tag="bank%d" % u) for u in range(PACK)]
+        old_half = [keep.tile([P, H], F32, name="old_half%d" % u, tag="a_row%d" % u) for u in range(PACK)]
+        for u in range(PACK):
+            nc.scalar.activation(old_half[u][:], page[u][:].indirect(n3_l[:]), ACT.Copy, scale=0.5)
+            quantize(z_q, blocks[u], z_g[:, u, :, :].rearrange("p m t -> p (m t)"))
+            product(cv_acc[u][:], z_q, blocks[u], z2_q, whole)
+        for u in range(PACK):
+            new = keep.tile([P, H], F32, name="new%d" % u)
+            nc.vector.scalar_tensor_tensor(new[:], cv_acc[u][:], 0.0625, old_half[u][:], ALU.mult, ALU.max)
+            nc.vector.tensor_copy(page[u][:].indirect(n3_l[:]), new[:])
+            nc.sync.dma_start(out.rearrange("(p u) w -> u p w", u=PACK)[u], page[u][:])

@@ -16,6 +16,7 @@ P = 128
 PACK = 4
 K, T, S, H, U = 512, 2048, 512, 512, 1024
 HALF = H // 2
+V_FETCH = 4
 FLOPS = 2 * (2 * K * S * H + S * H * H)
 
 
@@ -32,7 +33,7 @@ def tile_picked_momttriebpagex_none_p_kernel(tc, x_words, x_scales, wa, wb, gt, 
             return tile
 
         def load_weight_half(w, h, name):
-            raw = keep.tile([P, PACK, HALF], F32, name=name)
+            raw = keep.tile([P, PACK, HALF], F32, name=name, tag=name)
             nc.sync.dma_start(raw[:], w.rearrange("(p j) c -> p j c", j=PACK)[:, :, h * HALF:(h + 1) * HALF])
             return raw
 
@@ -46,7 +47,7 @@ def tile_picked_momttriebpagex_none_p_kernel(tc, x_words, x_scales, wa, wb, gt, 
         two_l = load_list(two, "two_l")
         offs_l = load_list(offs, "offs_l")
         for q in range(4):
-            nc.scalar.dma_start(scales_in[32 * q:32 * q + 4, :].bitcast(I32), x_scales[0, 4 * q:4 * q + 4, :].bitcast(I32))
+            (nc.scalar, nc.sync)[q % 2].dma_start(scales_in[32 * q:32 * q + 4, :].bitcast(I32), x_scales[0, 4 * q:4 * q + 4, :].bitcast(I32))
         words_in = keep.tile([P, T], U32, name="words_in", align_bytes=64)
         nc.sync.dma_start(words_in[:].bitcast(I32), x_words[0].rearrange("p n t -> p (n t)").bitcast(I32))
         wb_raw = [load_weight_half(wb, h, "wb_raw%d" % h) for h in range(2)]
@@ -74,7 +75,7 @@ def tile_picked_momttriebpagex_none_p_kernel(tc, x_words, x_scales, wa, wb, gt, 
             return grouped
 
         def mx_pair(name):
-            return (keep.tile([P, H], U32, name=name + "_codes", align_bytes=64),
+            return (keep.tile([P, H], U32, name=name + "_codes", tag=name + "_codes", align_bytes=64),
                     keep.tile([P, H], U8, name=name + "_scales", align_bytes=64))
 
         def quantize(pair, cols, grouped):
@@ -92,7 +93,7 @@ def tile_picked_momttriebpagex_none_p_kernel(tc, x_words, x_scales, wa, wb, gt, 
         xa_scales = pick(scales_in, U8, offs_l, "xa_scales")
         xb = (pick(words_in, U32, two_l, "xb_words"), xb_scales)
         wb_q = mx_pair("wb")
-        wb_g = [interleave(nc.scalar.copy, wb_raw[0][:], "wb_g0"), interleave(nc.vector.tensor_copy, wb_raw[1][:], "wb_g1")]
+        wb_g = [interleave(nc.scalar.copy, wb_raw[0][:], "wb_g0"), interleave(nc.scalar.copy, wb_raw[1][:], "wb_g1")]
         for h in range(2):
             nc.vector.quantize_mx(out=wb_q[0][:, halves[h]].bitcast(FP8X4), scales=wb_q[1][4 * h:P, halves[0]], in_=wb_g[h][:])
         b_acc = [psum.tile([P, H], F32, name="b_acc%d" % t, tag="bank%d" % t) for t in range(PACK)]
@@ -100,18 +101,17 @@ def tile_picked_momttriebpagex_none_p_kernel(tc, x_words, x_scales, wa, wb, gt, 
             for h in range(2):
                 nc.tensor.matmul_mx(out=b_acc[t][:, halves[h]], lhsT=xb[0][:, blocks[t]].bitcast(FP8X4), lhsT_scale=xb[1][:, blocks[t]],
                                     rhs=wb_q[0][:, halves[h]].bitcast(FP8X4), rhs_scale=wb_q[1][4 * h:P, halves[0]], start=True, stop=True)
-        xa = (pick(words_in, U32, offs_l, "xa_words", "wb_g1"), xa_scales)
+        xa = (pick(words_in, U32, offs_l, "xa_words"), xa_scales)
 
         b_row = [keep.tile([P, H], F32, name="b_row%d" % t) for t in range(PACK)]
         for t in range(PACK):
-            nc.scalar.copy(b_row[t][:], b_acc[t][:])
+            (nc.scalar.copy if t == 0 else nc.vector.tensor_copy)(b_row[t][:], b_acc[t][:])
 
         wa_q = mx_pair("wa")
-        wa_g = keep.tile([P, H * PACK], BF16, name="wa_g", tag="wb_g0", align_bytes=64)
         for h in range(2):
-            nc.vector.tensor_copy(wa_g[:, h * HALF * PACK:(h + 1) * HALF * PACK].rearrange("p (c i t) -> p c t i", i=4, t=PACK),
-                                  wa_raw[h][:].rearrange("p t (c i) -> p c t i", i=4))
-        quantize(wa_q, whole, wa_g[:])
+            wa_g = keep.tile([P, HALF * PACK], BF16, name="wa_g%d" % h, tag="wb_g%d" % (1 - h), align_bytes=64)
+            nc.gpsimd.tensor_copy(wa_g[:].rearrange("p (c t) -> p c t", t=PACK), wa_raw[h][:].rearrange("p t c -> p c t"))
+            quantize(wa_q, halves[h], wa_g[:])
         a_acc = [psum.tile([P, H], F32, name="a_acc%d" % t, tag="bank%d" % (PACK + t)) for t in range(PACK)]
         for t in range(PACK):
             product(a_acc[t][:], xa, blocks[t], wa_q, whole)
@@ -119,53 +119,58 @@ def tile_picked_momttriebpagex_none_p_kernel(tc, x_words, x_scales, wa, wb, gt, 
         def fetch(on_vector, dst, row, offsets, h):
             window = row[:].indirect(offsets[:, 16 * h:16 * (h + 1)])
             if on_vector:
-                nc.vector.tensor_copy(dst[:, halves[h]], window)
+                nc.vector.tensor_copy(dst, window)
             else:
-                nc.scalar.activation(dst[:, halves[h]], window, ACT.Copy)
+                nc.scalar.activation(dst, window, ACT.Copy)
 
         gate = keep.tile([P, PACK, H], F32, name="gate")
-        z2_rows = keep.tile([P, PACK, H], BF16, name="z2_rows")
-        b_sum = [keep.tile([P, H], F32, name="b_sum%d" % t) for t in range(PACK)]
+        z2_rows = keep.tile([P, PACK, H], BF16, name="z2_rows", tag="wa_raw1")
+        b_got = [keep.tile([P, H], F32, name="b_got%d" % t) for t in range(PACK)]
+        b_slot = ("wb_g1", "wb_g0", "xa_words", "wa_codes")
+        b_sum = [keep.tile([P, H], F32, name="b_sum%d" % t, tag=b_slot[t], align_bytes=64) for t in range(PACK)]
         a_row = [keep.tile([P, H], F32, name="a_row%d" % t, tag="a_row%d" % t) for t in range(PACK)]
-        for t in range(2):
-            for h in range(2):
-                fetch(False, b_sum[t], b_row[t], n2_l, h)
-            for h in range(2):
-                fetch(True, b_sum[t + 2], b_row[t + 2], n2_l, h)
-            nc.vector.tensor_tensor(b_sum[t][:], b_acc[t][:], b_sum[t][:], ALU.add)
-        for t in range(2, PACK):
-            nc.vector.tensor_tensor(b_sum[t][:], b_acc[t][:], b_sum[t][:], ALU.add)
         for t in range(PACK):
-            nc.scalar.activation(a_row[t][:], a_acc[t][:], ACT.Copy, scale=gt_t[:, t:t + 1])
+            for h in range(2):
+                fetch(False, b_got[t][:, halves[h]], b_row[t], n2_l, h)
+        for t in range(2):
+            nc.vector.tensor_tensor(b_sum[t][:], b_acc[t][:], b_got[t][:], ALU.add)
+        for t in range(PACK):
+            nc.vector.tensor_scalar(a_row[t][:], a_acc[t][:], gt_t[:, t:t + 1], None, ALU.mult)
+        for t in range(2, PACK):
+            nc.vector.tensor_tensor(b_sum[t][:], b_acc[t][:], b_got[t][:], ALU.add)
         for t in range(PACK):
             nc.scalar.activation(gate[:, t, :], b_sum[t][:], ACT.Sigmoid)
         for t in range(PACK):
-            nc.vector.tensor_scalar(z2_rows[:, t, :], b_row[t][:], gi_t[:, t:t + 1], None, ALU.mult)
-        z2_g = interleave(nc.vector.tensor_copy, z2_rows[:], "z2_g")
+            nc.gpsimd.tensor_scalar(z2_rows[:, t, :], b_row[t][:], gi_t[:, t:t + 1], 0.0, ALU.mult, ALU.add)
+        z2_g = keep.tile([P, H * PACK], BF16, name="z2_g", align_bytes=64)
+        nc.gpsimd.tensor_copy(z2_g[:].rearrange("p (c t) -> p c t", t=PACK), z2_rows[:].rearrange("p t c -> p c t"))
         z2_q = mx_pair("z2")
         quantize(z2_q, whole, z2_g[:])
 
-        a_got = [keep.tile([P, H], F32, name="a_got%d" % t) for t in range(PACK)]
-        a_sum = keep.tile([P, PACK, H], F32, name="a_sum")
         z_g = keep.tile([P, PACK, P, PACK], BF16, name="z_g", align_bytes=64)
+        got_v = keep.tile([P, V_FETCH, HALF], F32, name="got_v")
+        got_s = keep.tile([P, 2 * PACK - V_FETCH, HALF], F32, name="got_s", tag=b_slot[3], align_bytes=64)
         for h in range(2):
+            a_sum = keep.tile([P, PACK, HALF], F32, name="a_sum%d" % h, tag="a_sum")
             for t in range(PACK):
-                fetch(h == 0 and t == 0, a_got[t], a_row[t], n1_l, h)
-                nc.vector.scalar_tensor_tensor(a_sum[:, t, halves[h]], a_acc[t][:, halves[h]], gt_t[:, t:t + 1],
-                                               a_got[t][:, halves[h]], ALU.mult, ALU.add)
+                n = PACK * h + t
+                a_got = got_v[:, n, :] if n < V_FETCH else got_s[:, n - V_FETCH, :]
+                fetch(n < V_FETCH, a_got, a_row[t], n1_l, h)
+                nc.vector.scalar_tensor_tensor(a_sum[:, t, :], a_acc[t][:, halves[h]], gt_t[:, t:t + 1],
+                                               a_got, ALU.mult, ALU.add)
             nc.vector.tensor_tensor(z_g[:, :, 64 * h:64 * (h + 1), :].rearrange("p u m t -> p m t u"),
-                                    a_sum[:, :, halves[h]].rearrange("p t (m u) -> p m t u", u=PACK),
+                                    a_sum[:].rearrange("p t (m u) -> p m t u", u=PACK),
                                     gate[:, :, halves[h]].rearrange("p t (m u) -> p m t u", u=PACK), ALU.mult)
 
         z_q = mx_pair("z")
         cv_acc = [psum.tile([P, H], F32, name="cv_acc%d" % u, tag="bank%d" % u) for u in range(PACK)]
-        old_half = [keep.tile([P, H], F32, name="old_half%d" % u, tag="a_row%d" % u) for u in range(PACK)]
+        old_half = keep.tile([P, PACK, H], F32, name="old_half", tag="a_row3")
         for u in range(PACK):
-            nc.scalar.activation(old_half[u][:], page[u][:].indirect(n3_l[:]), ACT.Copy, scale=0.5)
+            nc.scalar.activation(old_half[:, u, :], page[u][:].indirect(n3_l[:]), ACT.Copy, scale=0.5)
             quantize(z_q, blocks[u], z_g[:, u, :, :].rearrange("p m t -> p (m t)"))
             product(cv_acc[u][:], z_q, blocks[u], z2_q, whole)
         for u in range(PACK):
             new = keep.tile([P, H], F32, name="new%d" % u)
-            nc.vector.scalar_tensor_tensor(new[:], cv_acc[u][:], 0.0625, old_half[u][:], ALU.mult, ALU.max)
+            nc.vector.scalar_tensor_tensor(new[:], cv_acc[u][:], 0.0625, old_half[:, u, :], ALU.mult, ALU.max)
             nc.vector.tensor_copy(page[u][:].indirect(n3_l[:]), new[:])
             nc.sync.dma_start(out.rearrange("(p u) w -> u p w", u=PACK)[u], page[u][:])

@@ -16,7 +16,6 @@ P = 128
 PACK = 4
 K, T, S, H, U = 512, 2048, 512, 512, 1024
 HALF = H // 2
-V_FETCH = 4
 FLOPS = 2 * (2 * K * S * H + S * H * H)
 
 
@@ -33,28 +32,31 @@ def tile_picked_momttriebpagex_none_p_kernel(tc, x_words, x_scales, wa, wb, gt, 
             return tile
 
         def load_weight_half(w, h, name):
-            raw = keep.tile([P, PACK, HALF], F32, name=name, tag=name)
+            raw = keep.tile([P, PACK, HALF], F32, name=name, tag=name, align_bytes=64)
             nc.sync.dma_start(raw[:], w.rearrange("(p j) c -> p j c", j=PACK)[:, :, h * HALF:(h + 1) * HALF])
             return raw
 
-        def load_column(v, name):
-            tile = keep.tile([P, PACK], F32, name=name)
-            nc.sync.dma_start(tile[:], v.rearrange("(p t) o -> p (t o)", t=PACK))
-            return tile
+        def load_column(queue, tile, v):
+            queue.dma_start(tile[:], v.rearrange("(p t) o -> p (t o)", t=PACK))
 
         scales_in = keep.tile([P, T], U8, name="scales_in", align_bytes=64)
-        nc.vector.memset(scales_in[:].bitcast(I32), 0)
+        nc.vector.memset(scales_in[:, :T // 2].bitcast(I32), 0)
+        nc.gpsimd.memset(scales_in[:, T // 2:].bitcast(I32), 0)
         two_l = load_list(two, "two_l")
         offs_l = load_list(offs, "offs_l")
         for q in range(4):
             (nc.scalar, nc.sync)[q % 2].dma_start(scales_in[32 * q:32 * q + 4, :].bitcast(I32), x_scales[0, 4 * q:4 * q + 4, :].bitcast(I32))
+        gi_t = keep.tile([P, PACK], F32, name="gi_t")
+        gt_t = keep.tile([P, PACK], F32, name="gt_t")
+        load_column(nc.scalar, gi_t, gi)
+        warm_out = keep.tile([P, 1], F32, name="warm_out")
+        nc.scalar.activation(warm_out[:], gi_t[:, 0:1], ACT.Sigmoid)
         words_in = keep.tile([P, T], U32, name="words_in", align_bytes=64)
         nc.sync.dma_start(words_in[:].bitcast(I32), x_words[0].rearrange("p n t -> p (n t)").bitcast(I32))
         wb_raw = [load_weight_half(wb, h, "wb_raw%d" % h) for h in range(2)]
         wa_raw = [load_weight_half(wa, h, "wa_raw%d" % h) for h in range(2)]
         n2_l = load_list(n2, "n2_l")
-        gi_t = load_column(gi, "gi_t")
-        gt_t = load_column(gt, "gt_t")
+        load_column(nc.sync, gt_t, gt)
         n1_l = load_list(n1, "n1_l")
         n3_l = load_list(n3, "n3_l")
         page = []
@@ -93,7 +95,7 @@ def tile_picked_momttriebpagex_none_p_kernel(tc, x_words, x_scales, wa, wb, gt, 
         xa_scales = pick(scales_in, U8, offs_l, "xa_scales")
         xb = (pick(words_in, U32, two_l, "xb_words"), xb_scales)
         wb_q = mx_pair("wb")
-        wb_g = [interleave(nc.scalar.copy, wb_raw[0][:], "wb_g0"), interleave(nc.scalar.copy, wb_raw[1][:], "wb_g1")]
+        wb_g = [interleave(nc.scalar.copy, wb_raw[0][:], "wb_g0"), interleave(nc.vector.tensor_copy, wb_raw[1][:], "wb_g1")]
         for h in range(2):
             nc.vector.quantize_mx(out=wb_q[0][:, halves[h]].bitcast(FP8X4), scales=wb_q[1][4 * h:P, halves[0]], in_=wb_g[h][:])
         b_acc = [psum.tile([P, H], F32, name="b_acc%d" % t, tag="bank%d" % t) for t in range(PACK)]
@@ -101,7 +103,7 @@ def tile_picked_momttriebpagex_none_p_kernel(tc, x_words, x_scales, wa, wb, gt, 
             for h in range(2):
                 nc.tensor.matmul_mx(out=b_acc[t][:, halves[h]], lhsT=xb[0][:, blocks[t]].bitcast(FP8X4), lhsT_scale=xb[1][:, blocks[t]],
                                     rhs=wb_q[0][:, halves[h]].bitcast(FP8X4), rhs_scale=wb_q[1][4 * h:P, halves[0]], start=True, stop=True)
-        xa = (pick(words_in, U32, offs_l, "xa_words"), xa_scales)
+        xa = (pick(words_in, U32, offs_l, "xa_words", "wb_g1"), xa_scales)
 
         b_row = [keep.tile([P, H], F32, name="b_row%d" % t) for t in range(PACK)]
         for t in range(PACK):
@@ -109,7 +111,7 @@ def tile_picked_momttriebpagex_none_p_kernel(tc, x_words, x_scales, wa, wb, gt, 
 
         wa_q = mx_pair("wa")
         for h in range(2):
-            wa_g = keep.tile([P, HALF * PACK], BF16, name="wa_g%d" % h, tag="wb_g%d" % (1 - h), align_bytes=64)
+            wa_g = keep.tile([P, HALF * PACK], BF16, name="wa_g%d" % h, tag=("wb_g0", "wb_raw1")[h], align_bytes=64)
             nc.gpsimd.tensor_copy(wa_g[:].rearrange("p (c t) -> p c t", t=PACK), wa_raw[h][:].rearrange("p t c -> p c t"))
             quantize(wa_q, halves[h], wa_g[:])
         a_acc = [psum.tile([P, H], F32, name="a_acc%d" % t, tag="bank%d" % (PACK + t)) for t in range(PACK)]
@@ -124,44 +126,55 @@ def tile_picked_momttriebpagex_none_p_kernel(tc, x_words, x_scales, wa, wb, gt, 
                 nc.scalar.activation(dst, window, ACT.Copy)
 
         gate = keep.tile([P, PACK, H], F32, name="gate")
-        z2_rows = keep.tile([P, PACK, H], BF16, name="z2_rows", tag="wa_raw1")
-        b_got = [keep.tile([P, H], F32, name="b_got%d" % t) for t in range(PACK)]
-        b_slot = ("wb_g1", "wb_g0", "xa_words", "wa_codes")
-        b_sum = [keep.tile([P, H], F32, name="b_sum%d" % t, tag=b_slot[t], align_bytes=64) for t in range(PACK)]
+        z2_rows = keep.tile([P, PACK, H], BF16, name="z2_rows", tag="wa_raw0", align_bytes=64)
+        b_got = [keep.tile([P, H], F32, name="b_got%d" % t, tag="b_got%d" % t, align_bytes=64) for t in range(PACK)]
+        b_sum_v = keep.tile([P, 2, H], F32, name="b_sum_v", tag="wb_raw1", align_bytes=64)
+        b_sum_g = keep.tile([P, 2, H], F32, name="b_sum_g", tag="wa_raw1", align_bytes=64)
+        b_sum = [b_sum_v[:, 0, :], b_sum_v[:, 1, :], b_sum_g[:, 0, :], b_sum_g[:, 1, :]]
         a_row = [keep.tile([P, H], F32, name="a_row%d" % t, tag="a_row%d" % t) for t in range(PACK)]
         for t in range(PACK):
             for h in range(2):
                 fetch(False, b_got[t][:, halves[h]], b_row[t], n2_l, h)
+
+        def weigh_b(t):
+            nc.gpsimd.tensor_scalar(z2_rows[:, t, :], b_row[t][:], gi_t[:, t:t + 1], 0.0, ALU.mult, ALU.add)
+
         for t in range(2):
-            nc.vector.tensor_tensor(b_sum[t][:], b_acc[t][:], b_got[t][:], ALU.add)
+            nc.vector.tensor_tensor(b_sum[t], b_acc[t][:], b_got[t][:], ALU.add)
+        for t in range(PACK):
+            weigh_b(t)
+        for t in range(2, PACK):
+            nc.gpsimd.tensor_tensor(b_sum[t], b_row[t][:], b_got[t][:], ALU.add)
         for t in range(PACK):
             nc.vector.tensor_scalar(a_row[t][:], a_acc[t][:], gt_t[:, t:t + 1], None, ALU.mult)
-        for t in range(2, PACK):
-            nc.vector.tensor_tensor(b_sum[t][:], b_acc[t][:], b_got[t][:], ALU.add)
-        for t in range(PACK):
-            nc.scalar.activation(gate[:, t, :], b_sum[t][:], ACT.Sigmoid)
-        for t in range(PACK):
-            nc.gpsimd.tensor_scalar(z2_rows[:, t, :], b_row[t][:], gi_t[:, t:t + 1], 0.0, ALU.mult, ALU.add)
-        z2_g = keep.tile([P, H * PACK], BF16, name="z2_g", align_bytes=64)
+        for t in range(2):
+            nc.scalar.activation(gate[:, t, :], b_sum[t], ACT.Sigmoid)
+        z2_g = keep.tile([P, H * PACK], BF16, name="z2_g", tag="b_got3", align_bytes=64)
         nc.gpsimd.tensor_copy(z2_g[:].rearrange("p (c t) -> p c t", t=PACK), z2_rows[:].rearrange("p t c -> p c t"))
-        z2_q = mx_pair("z2")
-        quantize(z2_q, whole, z2_g[:])
 
         z_g = keep.tile([P, PACK, P, PACK], BF16, name="z_g", align_bytes=64)
-        got_v = keep.tile([P, V_FETCH, HALF], F32, name="got_v")
-        got_s = keep.tile([P, 2 * PACK - V_FETCH, HALF], F32, name="got_s", tag=b_slot[3], align_bytes=64)
+        got_v = keep.tile([P, 2, HALF], F32, name="got_v")
+        got_s = keep.tile([P, 2, HALF], F32, name="got_s", tag="wb_raw1", align_bytes=64)
+        got_late = keep.tile([P, PACK, HALF], F32, name="got_late", tag="wa_raw1", align_bytes=64)
+        got = [[got_v[:, 0, :], got_v[:, 1, :], got_s[:, 0, :], got_s[:, 1, :]], [got_late[:, t, :] for t in range(PACK)]]
         for h in range(2):
             a_sum = keep.tile([P, PACK, HALF], F32, name="a_sum%d" % h, tag="a_sum")
+            a_got = got[h]
             for t in range(PACK):
-                n = PACK * h + t
-                a_got = got_v[:, n, :] if n < V_FETCH else got_s[:, n - V_FETCH, :]
-                fetch(n < V_FETCH, a_got, a_row[t], n1_l, h)
+                fetch(h == 0 and t < 2, a_got[t], a_row[t], n1_l, h)
+            if h == 0:
+                for t in range(2, PACK):
+                    nc.scalar.activation(gate[:, t, :], b_sum[t], ACT.Sigmoid)
+            for t in range(PACK):
                 nc.vector.scalar_tensor_tensor(a_sum[:, t, :], a_acc[t][:, halves[h]], gt_t[:, t:t + 1],
-                                               a_got, ALU.mult, ALU.add)
+                                               a_got[t], ALU.mult, ALU.add)
             nc.vector.tensor_tensor(z_g[:, :, 64 * h:64 * (h + 1), :].rearrange("p u m t -> p m t u"),
                                     a_sum[:].rearrange("p t (m u) -> p m t u", u=PACK),
                                     gate[:, :, halves[h]].rearrange("p t (m u) -> p m t u", u=PACK), ALU.mult)
 
+        z2_q = (keep.tile([P, H], U32, name="z2_codes", tag="wa_raw1", align_bytes=64),
+                keep.tile([P, H], U8, name="z2_scales", align_bytes=64))
+        quantize(z2_q, whole, z2_g[:])
         z_q = mx_pair("z")
         cv_acc = [psum.tile([P, H], F32, name="cv_acc%d" % u, tag="bank%d" % u) for u in range(PACK)]
         old_half = keep.tile([P, PACK, H], F32, name="old_half", tag="a_row3")
@@ -169,8 +182,14 @@ def tile_picked_momttriebpagex_none_p_kernel(tc, x_words, x_scales, wa, wb, gt, 
             nc.scalar.activation(old_half[:, u, :], page[u][:].indirect(n3_l[:]), ACT.Copy, scale=0.5)
             quantize(z_q, blocks[u], z_g[:, u, :, :].rearrange("p m t -> p (m t)"))
             product(cv_acc[u][:], z_q, blocks[u], z2_q, whole)
+        new = [keep.tile([P, H], F32, name="new%d" % u) for u in range(PACK)]
+
+        def larger(u):
+            nc.vector.scalar_tensor_tensor(new[u][:], cv_acc[u][:], 0.0625, old_half[:, u, :], ALU.mult, ALU.max)
+
+        larger(0)
         for u in range(PACK):
-            new = keep.tile([P, H], F32, name="new%d" % u)
-            nc.vector.scalar_tensor_tensor(new[:], cv_acc[u][:], 0.0625, old_half[:, u, :], ALU.mult, ALU.max)
-            nc.vector.tensor_copy(page[u][:].indirect(n3_l[:]), new[:])
+            if u + 1 < PACK:
+                larger(u + 1)
+            nc.vector.tensor_copy(page[u][:].indirect(n3_l[:]), new[u][:])
             nc.sync.dma_start(out.rearrange("(p u) w -> u p w", u=PACK)[u], page[u][:])

@@ -1,6 +1,7 @@
 from contextlib import ExitStack
 
 import concourse.mybir as mybir
+from concourse.masks import make_identity
 
 F32 = mybir.dt.float32
 BF16 = mybir.dt.bfloat16
@@ -16,6 +17,7 @@ P = 128
 PACK = 4
 K, T, S, H, U = 512, 2048, 512, 512, 1024
 HALF = H // 2
+DIRECT = 2
 FLOPS = 2 * (2 * K * S * H + S * H * H)
 
 
@@ -42,6 +44,8 @@ def tile_picked_momttriebpagex_none_p_kernel(tc, x_words, x_scales, wa, wb, gt, 
         scales_in = keep.tile([P, T], U8, name="scales_in", align_bytes=64)
         nc.vector.memset(scales_in[:, :T // 2].bitcast(I32), 0)
         nc.gpsimd.memset(scales_in[:, T // 2:].bitcast(I32), 0)
+        identity = keep.tile([P, P], F32, name="identity")
+        make_identity(nc, identity[:])
         two_l = load_list(two, "two_l")
         offs_l = load_list(offs, "offs_l")
         for q in range(4):
@@ -176,20 +180,41 @@ def tile_picked_momttriebpagex_none_p_kernel(tc, x_words, x_scales, wa, wb, gt, 
                 keep.tile([P, H], U8, name="z2_scales", align_bytes=64))
         quantize(z2_q, whole, z2_g[:])
         z_q = mx_pair("z")
-        cv_acc = [psum.tile([P, H], F32, name="cv_acc%d" % u, tag="bank%d" % u) for u in range(PACK)]
         old_half = keep.tile([P, PACK, H], F32, name="old_half", tag="a_row3")
+        cv_acc = []
         for u in range(PACK):
             nc.scalar.activation(old_half[:, u, :], page[u][:].indirect(n3_l[:]), ACT.Copy, scale=0.5)
             quantize(z_q, blocks[u], z_g[:, u, :, :].rearrange("p m t -> p (m t)"))
-            product(cv_acc[u][:], z_q, blocks[u], z2_q, whole)
-        new = [keep.tile([P, H], F32, name="new%d" % u) for u in range(PACK)]
+            acc = psum.tile([P, H], F32, name="cv_acc%d" % u, tag="bank%d" % u)
+            if u < DIRECT:
+                product(acc[:], z_q, blocks[u], z2_q, whole)
+            else:
+                for j in range(PACK):
+                    product(acc[:, blocks[j]], z2_q, blocks[j], z_q, blocks[u])
+            cv_acc.append(acc)
 
-        def larger(u):
-            nc.vector.scalar_tensor_tensor(new[u][:], cv_acc[u][:], 0.0625, old_half[:, u, :], ALU.mult, ALU.max)
-
-        larger(0)
-        for u in range(PACK):
-            if u + 1 < PACK:
-                larger(u + 1)
-            nc.vector.tensor_copy(page[u][:].indirect(n3_l[:]), new[u][:])
+        def store(u):
             nc.sync.dma_start(out.rearrange("(p u) w -> u p w", u=PACK)[u], page[u][:])
+
+        new = [keep.tile([P, H], F32, name="new%d" % u) for u in range(PACK)]
+        for u in range(DIRECT):
+            nc.vector.scalar_tensor_tensor(new[u][:], cv_acc[u][:], 0.0625, old_half[:, u, :], ALU.mult, ALU.max)
+        for u in range(DIRECT, PACK):
+            cv_t = keep.tile([P, H], F32, name="cv_t%d" % u)
+            nc.scalar.activation(cv_t[:], cv_acc[u][:], ACT.Copy, scale=0.0625)
+            old_acc = psum.tile([P, H], F32, name="old_acc%d" % u, tag="bank%d" % (u - DIRECT))
+            for j in range(PACK):
+                nc.tensor.transpose(old_acc[:, blocks[j]], old_half[:, u, blocks[j]], identity[:])
+            old_t = keep.tile([P, H], F32, name="old_t%d" % u)
+            nc.scalar.activation(old_t[:], old_acc[:], ACT.Copy, scale=-1.0)
+            excess = psum.tile([P, H], F32, name="excess%d" % u, tag="bank%d" % (PACK + u))
+            for j in range(PACK):
+                nc.tensor.matmul(excess[:, blocks[j]], cv_t[:, blocks[j]], identity[:], is_transpose=True, start=True, stop=False)
+                nc.tensor.matmul(excess[:, blocks[j]], old_t[:, blocks[j]], identity[:], is_transpose=True, start=False, stop=True)
+            nc.scalar.activation(new[u][:], excess[:], ACT.Relu)
+        for u in range(PACK):
+            if u < DIRECT:
+                nc.vector.tensor_copy(page[u][:].indirect(n3_l[:]), new[u][:])
+            else:
+                nc.vector.tensor_tensor(page[u][:].indirect(n3_l[:]), new[u][:], old_half[:, u, :], ALU.add)
+            store(u)

from contextlib import ExitStack

import concourse.mybir as mybir
from concourse.masks import make_identity

F32 = mybir.dt.float32
BF16 = mybir.dt.bfloat16
I32 = mybir.dt.int32
U32 = mybir.dt.uint32
U16 = mybir.dt.uint16
U8 = mybir.dt.uint8
FP8X4 = mybir.dt.float8_e4m3fn_x4
ALU = mybir.AluOpType
ACT = mybir.ActivationFunctionType

P = 128
PACK = 4
K, T, S, H, U = 512, 2048, 512, 512, 1024
HALF = H // 2
DIRECT = 2
FLOPS = 2 * (2 * K * S * H + S * H * H)


def tile_picked_momttriebpagex_none_p_kernel(tc, x_words, x_scales, wa, wb, gt, gi, mem, offs, two, n1, n2, n3, out):
    nc = tc.nc
    with ExitStack() as ctx:
        lists = ctx.enter_context(tc.tile_pool(name="lists", bufs=1))
        keep = ctx.enter_context(tc.tile_pool(name="keep", bufs=1))
        psum = ctx.enter_context(tc.psum_pool(name="psum", bufs=1))

        def load_list(src, name):
            tile = lists.tile([P, S // 16], U16, name=name)
            nc.sync.dma_start(tile[:], src)
            return tile

        def load_weight_half(w, h, name):
            raw = keep.tile([P, PACK, HALF], F32, name=name, tag=name, align_bytes=64)
            nc.sync.dma_start(raw[:], w.rearrange("(p j) c -> p j c", j=PACK)[:, :, h * HALF:(h + 1) * HALF])
            return raw

        def load_column(queue, tile, v):
            queue.dma_start(tile[:], v.rearrange("(p t) o -> p (t o)", t=PACK))

        scales_in = keep.tile([P, T], U8, name="scales_in", align_bytes=64)
        nc.vector.memset(scales_in[:, :T // 2].bitcast(I32), 0)
        nc.gpsimd.memset(scales_in[:, T // 2:].bitcast(I32), 0)
        identity = keep.tile([P, P], F32, name="identity")
        make_identity(nc, identity[:])
        two_l = load_list(two, "two_l")
        offs_l = load_list(offs, "offs_l")
        for q in range(4):
            (nc.scalar, nc.sync)[q % 2].dma_start(scales_in[32 * q:32 * q + 4, :].bitcast(I32), x_scales[0, 4 * q:4 * q + 4, :].bitcast(I32))
        gi_t = keep.tile([P, PACK], F32, name="gi_t")
        gt_t = keep.tile([P, PACK], F32, name="gt_t")
        load_column(nc.scalar, gi_t, gi)
        warm_out = keep.tile([P, 1], F32, name="warm_out")
        nc.scalar.activation(warm_out[:], gi_t[:, 0:1], ACT.Sigmoid)
        words_in = keep.tile([P, T], U32, name="words_in", align_bytes=64)
        nc.sync.dma_start(words_in[:].bitcast(I32), x_words[0].rearrange("p n t -> p (n t)").bitcast(I32))
        wb_raw = [load_weight_half(wb, h, "wb_raw%d" % h) for h in range(2)]
        wa_raw = [load_weight_half(wa, h, "wa_raw%d" % h) for h in range(2)]
        n2_l = load_list(n2, "n2_l")
        load_column(nc.sync, gt_t, gt)
        n1_l = load_list(n1, "n1_l")
        n3_l = load_list(n3, "n3_l")
        page = []
        for u in range(PACK):
            tile = keep.tile([P, U], F32, name="page%d" % u)
            nc.sync.dma_start(tile[:], mem.rearrange("(p u) w -> u p w", u=PACK)[u])
            page.append(tile)

        def pick(table, dtype, offsets, name, tag=None):
            picked = keep.tile([P, S], dtype, name=name, tag=tag or name, align_bytes=64)
            nc.vector.tensor_copy(picked[:].rearrange("p (t m) -> p m t", t=PACK), table[:].indirect(offsets[:]))
            return picked

        def interleave(copy, src, name, tag=None):
            width = src.shape[2]
            grouped = keep.tile([P, width * PACK], BF16, name=name, tag=tag or name, align_bytes=64)
            copy(grouped[:].rearrange("p (c i t) -> p c t i", i=4, t=PACK), src.rearrange("p t (c i) -> p c t i", i=4))
            return grouped

        def mx_pair(name):
            return (keep.tile([P, H], U32, name=name + "_codes", tag=name + "_codes", align_bytes=64),
                    keep.tile([P, H], U8, name=name + "_scales", align_bytes=64))

        def quantize(pair, cols, grouped):
            nc.vector.quantize_mx(out=pair[0][:, cols].bitcast(FP8X4), scales=pair[1][:, cols], in_=grouped)

        def product(acc, lhs, lhs_cols, rhs, rhs_cols):
            nc.tensor.matmul_mx(out=acc, lhsT=lhs[0][:, lhs_cols].bitcast(FP8X4), lhsT_scale=lhs[1][:, lhs_cols],
                                rhs=rhs[0][:, rhs_cols].bitcast(FP8X4), rhs_scale=rhs[1][:, rhs_cols], start=True, stop=True)

        halves = [slice(h * HALF, (h + 1) * HALF) for h in range(2)]
        blocks = [slice(t * P, (t + 1) * P) for t in range(PACK)]
        whole = slice(0, H)

        xb_scales = pick(scales_in, U8, two_l, "xb_scales")
        xa_scales = pick(scales_in, U8, offs_l, "xa_scales")
        xb = (pick(words_in, U32, two_l, "xb_words"), xb_scales)
        wb_q = mx_pair("wb")
        wb_g = [interleave(nc.scalar.copy, wb_raw[0][:], "wb_g0"), interleave(nc.vector.tensor_copy, wb_raw[1][:], "wb_g1")]
        for h in range(2):
            nc.vector.quantize_mx(out=wb_q[0][:, halves[h]].bitcast(FP8X4), scales=wb_q[1][4 * h:P, halves[0]], in_=wb_g[h][:])
        b_acc = [psum.tile([P, H], F32, name="b_acc%d" % t, tag="bank%d" % t) for t in range(PACK)]
        for t in range(PACK):
            for h in range(2):
                nc.tensor.matmul_mx(out=b_acc[t][:, halves[h]], lhsT=xb[0][:, blocks[t]].bitcast(FP8X4), lhsT_scale=xb[1][:, blocks[t]],
                                    rhs=wb_q[0][:, halves[h]].bitcast(FP8X4), rhs_scale=wb_q[1][4 * h:P, halves[0]], start=True, stop=True)
        xa = (pick(words_in, U32, offs_l, "xa_words", "wb_g1"), xa_scales)

        b_row = [keep.tile([P, H], F32, name="b_row%d" % t) for t in range(PACK)]
        for t in range(PACK):
            (nc.scalar.copy if t == 0 else nc.vector.tensor_copy)(b_row[t][:], b_acc[t][:])

        wa_q = mx_pair("wa")
        for h in range(2):
            wa_g = keep.tile([P, HALF * PACK], BF16, name="wa_g%d" % h, tag=("wb_g0", "wb_raw1")[h], align_bytes=64)
            nc.gpsimd.tensor_copy(wa_g[:].rearrange("p (c t) -> p c t", t=PACK), wa_raw[h][:].rearrange("p t c -> p c t"))
            quantize(wa_q, halves[h], wa_g[:])
        a_acc = [psum.tile([P, H], F32, name="a_acc%d" % t, tag="bank%d" % (PACK + t)) for t in range(PACK)]
        for t in range(PACK):
            product(a_acc[t][:], xa, blocks[t], wa_q, whole)

        def fetch(on_vector, dst, row, offsets, h):
            window = row[:].indirect(offsets[:, 16 * h:16 * (h + 1)])
            if on_vector:
                nc.vector.tensor_copy(dst, window)
            else:
                nc.scalar.activation(dst, window, ACT.Copy)

        gate = keep.tile([P, PACK, H], F32, name="gate")
        z2_rows = keep.tile([P, PACK, H], BF16, name="z2_rows", tag="wa_raw0", align_bytes=64)
        b_got = [keep.tile([P, H], F32, name="b_got%d" % t, tag="b_got%d" % t, align_bytes=64) for t in range(PACK)]
        b_sum_v = keep.tile([P, 2, H], F32, name="b_sum_v", tag="wb_raw1", align_bytes=64)
        b_sum_g = keep.tile([P, 2, H], F32, name="b_sum_g", tag="wa_raw1", align_bytes=64)
        b_sum = [b_sum_v[:, 0, :], b_sum_v[:, 1, :], b_sum_g[:, 0, :], b_sum_g[:, 1, :]]
        a_row = [keep.tile([P, H], F32, name="a_row%d" % t, tag="a_row%d" % t) for t in range(PACK)]
        for t in range(PACK):
            for h in range(2):
                fetch(False, b_got[t][:, halves[h]], b_row[t], n2_l, h)

        def weigh_b(t):
            nc.gpsimd.tensor_scalar(z2_rows[:, t, :], b_row[t][:], gi_t[:, t:t + 1], 0.0, ALU.mult, ALU.add)

        for t in range(2):
            nc.vector.tensor_tensor(b_sum[t], b_acc[t][:], b_got[t][:], ALU.add)
        for t in range(PACK):
            weigh_b(t)
        for t in range(2, PACK):
            nc.gpsimd.tensor_tensor(b_sum[t], b_row[t][:], b_got[t][:], ALU.add)
        for t in range(PACK):
            nc.vector.tensor_scalar(a_row[t][:], a_acc[t][:], gt_t[:, t:t + 1], None, ALU.mult)
        for t in range(2):
            nc.scalar.activation(gate[:, t, :], b_sum[t], ACT.Sigmoid)
        z2_g = keep.tile([P, H * PACK], BF16, name="z2_g", tag="b_got3", align_bytes=64)
        nc.gpsimd.tensor_copy(z2_g[:].rearrange("p (c t) -> p c t", t=PACK), z2_rows[:].rearrange("p t c -> p c t"))

        z_g = keep.tile([P, PACK, P, PACK], BF16, name="z_g", align_bytes=64)
        got_v = keep.tile([P, 2, HALF], F32, name="got_v")
        got_s = keep.tile([P, 2, HALF], F32, name="got_s", tag="wb_raw1", align_bytes=64)
        got_late = keep.tile([P, PACK, HALF], F32, name="got_late", tag="wa_raw1", align_bytes=64)
        got = [[got_v[:, 0, :], got_v[:, 1, :], got_s[:, 0, :], got_s[:, 1, :]], [got_late[:, t, :] for t in range(PACK)]]
        for h in range(2):
            a_sum = keep.tile([P, PACK, HALF], F32, name="a_sum%d" % h, tag="a_sum")
            a_got = got[h]
            for t in range(PACK):
                fetch(h == 0 and t < 2, a_got[t], a_row[t], n1_l, h)
            if h == 0:
                for t in range(2, PACK):
                    nc.scalar.activation(gate[:, t, :], b_sum[t], ACT.Sigmoid)
            for t in range(PACK):
                nc.vector.scalar_tensor_tensor(a_sum[:, t, :], a_acc[t][:, halves[h]], gt_t[:, t:t + 1],
                                               a_got[t], ALU.mult, ALU.add)
            nc.vector.tensor_tensor(z_g[:, :, 64 * h:64 * (h + 1), :].rearrange("p u m t -> p m t u"),
                                    a_sum[:].rearrange("p t (m u) -> p m t u", u=PACK),
                                    gate[:, :, halves[h]].rearrange("p t (m u) -> p m t u", u=PACK), ALU.mult)

        z2_q = (keep.tile([P, H], U32, name="z2_codes", tag="wa_raw1", align_bytes=64),
                keep.tile([P, H], U8, name="z2_scales", align_bytes=64))
        quantize(z2_q, whole, z2_g[:])
        z_q = mx_pair("z")
        old_half = keep.tile([P, PACK, H], F32, name="old_half", tag="a_row3")
        cv_acc = []
        for u in range(PACK):
            nc.scalar.activation(old_half[:, u, :], page[u][:].indirect(n3_l[:]), ACT.Copy, scale=0.5)
            quantize(z_q, blocks[u], z_g[:, u, :, :].rearrange("p m t -> p (m t)"))
            acc = psum.tile([P, H], F32, name="cv_acc%d" % u, tag="bank%d" % u)
            if u < DIRECT:
                product(acc[:], z_q, blocks[u], z2_q, whole)
            else:
                for j in range(PACK):
                    product(acc[:, blocks[j]], z2_q, blocks[j], z_q, blocks[u])
            cv_acc.append(acc)

        def store(u):
            nc.sync.dma_start(out.rearrange("(p u) w -> u p w", u=PACK)[u], page[u][:])

        new = [keep.tile([P, H], F32, name="new%d" % u) for u in range(PACK)]
        for u in range(DIRECT):
            nc.vector.scalar_tensor_tensor(new[u][:], cv_acc[u][:], 0.0625, old_half[:, u, :], ALU.mult, ALU.max)
        for u in range(DIRECT, PACK):
            cv_t = keep.tile([P, H], F32, name="cv_t%d" % u)
            nc.scalar.activation(cv_t[:], cv_acc[u][:], ACT.Copy, scale=0.0625)
            old_acc = psum.tile([P, H], F32, name="old_acc%d" % u, tag="bank%d" % (u - DIRECT))
            for j in range(PACK):
                nc.tensor.transpose(old_acc[:, blocks[j]], old_half[:, u, blocks[j]], identity[:])
            old_t = keep.tile([P, H], F32, name="old_t%d" % u)
            nc.scalar.activation(old_t[:], old_acc[:], ACT.Copy, scale=-1.0)
            excess = psum.tile([P, H], F32, name="excess%d" % u, tag="bank%d" % (PACK + u))
            for j in range(PACK):
                nc.tensor.matmul(excess[:, blocks[j]], cv_t[:, blocks[j]], identity[:], is_transpose=True, start=True, stop=False)
                nc.tensor.matmul(excess[:, blocks[j]], old_t[:, blocks[j]], identity[:], is_transpose=True, start=False, stop=True)
            nc.scalar.activation(new[u][:], excess[:], ACT.Relu)
        for u in range(PACK):
            if u < DIRECT:
                nc.vector.tensor_copy(page[u][:].indirect(n3_l[:]), new[u][:])
            else:
                nc.vector.tensor_tensor(page[u][:].indirect(n3_l[:]), new[u][:], old_half[:, u, :], ALU.add)
            store(u)
